import numpy as np
import ml_dtypes


def mxq(x, axis, fmt="e4m3"):
    dtype, down = {"e4m3": (ml_dtypes.float8_e4m3fn, 7), "e5m2": (ml_dtypes.float8_e5m2, 14)}[fmt]
    v = np.moveaxis(np.asarray(x, np.float32).astype(ml_dtypes.bfloat16).astype(np.float64), axis, -1)
    blocks = v.reshape(v.shape[:-1] + (-1, 32))
    amax = np.abs(blocks).max(-1, keepdims=True)
    byte = np.maximum(np.where(amax > 0, np.frexp(amax)[1] - 1 + 127, 0) - down, 1)
    scale = np.exp2(byte - 127.0)
    codes = (blocks / scale).astype(np.float32).astype(dtype).astype(np.float64)
    return np.moveaxis((codes * scale).reshape(v.shape), -1, axis)


WIDE = False


def mx_kscale(k):
    if not WIDE:
        return np.ones(k)
    levels = np.array([10, -10, 5, -5, 0])
    if k % 512:
        return np.exp2(np.random.permutation(np.resize(levels, k // 32))).repeat(32)
    a = np.empty((k // 512, 16))
    for p in range(k // 512):
        a[p, :8] = np.random.permutation(np.resize(levels, 8))
        for g in range(8):
            far = levels[np.abs(levels - a[p, g]) >= 10]
            a[p, g + 8] = far[np.random.randint(len(far))]
    return np.exp2(a.ravel()).repeat(32)


def f64(x):
    return np.asarray(x).astype(np.float64)


def striped(idx):
    return np.tile(idx.reshape(-1, 16).T, (8, 1)).astype(np.uint16)


def unstriped(offs):
    return offs[:16].T.reshape(-1).astype(np.int64)


E2M1 = np.array([0.0, 0.5, 1.0, 1.5, 2.0, 3.0, 4.0, 6.0, -0.0, -0.5, -1.0, -1.5, -2.0, -3.0, -4.0, -6.0])


def pack_weight(w, fmt):
    k, n = w.shape
    w = f64(np.asarray(w, np.float32).astype(ml_dtypes.bfloat16)).reshape(k // 32, 32, n)
    amax = np.abs(w).max(1)
    if fmt == "e4m3":
        byte = np.frexp(amax)[1] - 1 + 127 - 7
    else:
        mant, ex = np.frexp(amax / 6.0)
        byte = np.where(mant > 0.5, ex, ex - 1) + 127
    byte = np.clip(np.where(amax > 0, byte, 1), 1, 254)
    scaled = (w * np.exp2(127.0 - byte)[:, None, :]).reshape(k, n).astype(np.float32)
    by_word = np.ascontiguousarray(scaled.reshape(k // 512, 128, 4, n).transpose(0, 1, 3, 2))
    if fmt == "e4m3":
        words = by_word.astype(ml_dtypes.float8_e4m3fn).view(np.uint8)
    else:
        c = by_word.astype(ml_dtypes.float4_e2m1fn).view(np.uint8) & 0xF
        words = (c[..., 0::2] | (c[..., 1::2] << 4)).reshape(k // 512, 128, 2 * n)
    return np.ascontiguousarray(words), np.ascontiguousarray(byte.astype(np.uint8).reshape(k // 512, 16, n))


def unpack_weight(words, scales, fmt):
    g, _, n = scales.shape
    words = np.ascontiguousarray(words).reshape(g, 128, n, -1)
    if fmt == "e4m3":
        vals = words.view(ml_dtypes.float8_e4m3fn).astype(np.float64)
    else:
        nib = np.empty((g, 128, n, 4), np.uint8)
        nib[..., 0::2] = words & 0xF
        nib[..., 1::2] = words >> 4
        vals = E2M1[nib]
    vals = vals * np.repeat(np.exp2(scales.astype(np.float64) - 127.0), 8, axis=1)[..., None]
    return vals.transpose(0, 1, 3, 2).reshape(g * 512, n)


def gelu(v):
    return 0.5 * v * (1.0 + np.tanh(np.sqrt(2.0 / np.pi) * (v + 0.044715 * v**3)))


K1, K2, H, N, T, S, P = 1024, 512, 1024, 512, 2048, 1024, 512

def setup_inputs():
    n = np.random.standard_normal
    s1, s2, u = mx_kscale(K1)[:, None], mx_kscale(K2)[:, None], mx_kscale(H)[:, None]
    tab_words, tab_scales = pack_weight(n((K1, T)) * s1, "e4m3")
    tab2_words, tab2_scales = pack_weight(n((K2, T)) * s2, "e4m3")
    w2_words, w2_scales = pack_weight(n((K2, H)) / s2 / np.sqrt(K2), "e2m1")
    w4_words, w4_scales = pack_weight(1.4 * n((H, N)) / u / np.sqrt(H), "e2m1")
    perm = np.random.permutation(T)
    return {
        "tab_words": tab_words, "tab_scales": tab_scales,
        "tab2_words": tab2_words, "tab2_scales": tab2_scales,
        "offs": striped(np.random.permutation(T)[:S]),
        "offs2": striped(np.random.permutation(T)[:P]),
        "pos1": striped(np.random.permutation(S)[:P]),
        "offs3": striped(perm[:S]), "offs4": striped(perm[S:S + P]),
        "w1": (1.3 * n((K1, H)) / s1 / np.sqrt(K1)).astype(np.float32),
        "w2_words": w2_words, "w2_scales": w2_scales,
        "shift": (0.8 * n((H, P))).astype(np.float32),
        "gain": (np.exp(0.3 * n(H)) * u[:, 0]).astype(np.float32),
        "w3": (1.4 * n((H, N)) / u / np.sqrt(H)).astype(np.float32),
        "w4_words": w4_words, "w4_scales": w4_scales,
        "page1": n((N, T)).astype(np.float32),
        "wg1": np.exp(0.3 * n((128, S))).astype(np.float32),
        "wg2": np.exp(0.3 * n((128, P))).astype(np.float32)}

def reference(tab_words, tab_scales, tab2_words, tab2_scales, offs, offs2, pos1, offs3, offs4, w1, w2_words, w2_scales,
              shift, gain, w3, w4_words, w4_scales, page1, wg1, wg2):
    v = unpack_weight(tab_words, tab_scales, "e4m3")[:, unstriped(offs)]
    v2 = unpack_weight(tab2_words, tab2_scales, "e4m3")[:, unstriped(offs2)]
    h1 = mxq(f64(w1), 0, "e4m3").T @ v
    h2 = unpack_weight(w2_words, w2_scales, "e2m1").T @ v2
    z = np.zeros((H, S + P))
    z[:, :S] = h1
    z[:, S:] = h2 + h1[:, unstriped(pos1)] + f64(shift)
    z = np.tanh(z) * f64(gain)[:, None]
    y1 = mxq(f64(w3), 0, "e4m3").T @ mxq(z[:, :S], 0, "e4m3")
    y2 = unpack_weight(w4_words, w4_scales, "e2m1").T @ mxq(z[:, S:], 0, "e4m3")
    out = f64(page1).copy()
    out[:, unstriped(offs3)] = np.tile(f64(wg1), (N // 128, 1)) * y1
    out[:, unstriped(offs4)] = np.tile(f64(wg2), (N // 128, 1)) * y2
    return out

@@ -1,0 +1,277 @@
+from contextlib import ExitStack
+
+import concourse.mybir as mybir
+
+K1, K2, H, N, T, S, M = 1024, 512, 1024, 512, 2048, 1024, 512
+FLOPS = 2 * (K1 * H * S + K2 * H * M + H * N * S + H * N * M)
+
+F32 = mybir.dt.float32
+BF16 = mybir.dt.bfloat16
+I32 = mybir.dt.int32
+U32 = mybir.dt.uint32
+U16 = mybir.dt.uint16
+U8 = mybir.dt.uint8
+FP8X4 = mybir.dt.float8_e4m3fn_x4
+FP4X4 = mybir.dt.float4_e2m1fn_x4
+ADD = mybir.AluOpType.add
+MULT = mybir.AluOpType.mult
+TANH = mybir.ActivationFunctionType.Tanh
+COPY = mybir.ActivationFunctionType.Copy
+
+P = 128
+PACK = 4
+KP = P * PACK
+W = 512
+LC = W // 16
+
+
+def tile_list_trigger_features_kernel(
+    tc, tab_words, tab_scales, tab2_words, tab2_scales, offs, offs2, pos1, offs3, offs4,
+    w1, w2_words, w2_scales, shift, gain, w3, w4_words, w4_scales, page1, wg1, wg2, out,
+):
+    nc = tc.nc
+    with ExitStack() as ctx:
+        keep = ctx.enter_context(tc.tile_pool(name="keep", bufs=1))
+        wide = ctx.enter_context(tc.tile_pool(name="wide", bufs=6))
+        ring = ctx.enter_context(tc.tile_pool(name="ring", bufs=1))
+        psum = ctx.enter_context(tc.psum_pool(name="psum", bufs=1))
+
+        def held(name, shape, dtype):
+            return keep.tile(shape, dtype, name=name, align_bytes=64)
+
+        def load(name, shape, dtype, src):
+            t = held(name, shape, dtype)
+            nc.sync.dma_start(t[:], src)
+            return t
+
+        def load_wide(src):
+            t = wide.tile([P, PACK, W], F32, name="wide", align_bytes=64)
+            nc.sync.dma_start(t[:], src.rearrange("(p j) c -> p j c", j=PACK))
+            return t
+
+        def load_words(name, src):
+            t = held(name, [P, T], U32)
+            nc.sync.dma_start(t[:].bitcast(I32), src.rearrange("p t i -> p (t i)").bitcast(I32))
+            return t
+
+        tab_plane = held("tab_plane", [P, T], U8)
+        w2_plane = held("w2_plane", [P, H], U8)
+        tab2_plane = held("tab2_plane", [P, T], U8)
+        w4_plane = held("w4_plane", [P, 2, N], U8)
+        nc.gpsimd.memset(tab_plane[:].bitcast(I32), 0)
+        nc.vector.memset(w2_plane[:].bitcast(I32), 0)
+        nc.vector.memset(tab2_plane[:].bitcast(I32), 0)
+        nc.vector.memset(w4_plane[:].bitcast(I32), 0)
+        for q in range(4):
+            nc.gpsimd.dma_start(
+                w4_plane[32 * q : 32 * q + 4, :, :].bitcast(I32),
+                w4_scales[:, 4 * q : 4 * q + 4, :].rearrange("a r n -> r a n").bitcast(I32),
+            )
+
+        tab_w = [load_words("tab_w0", tab_words[0])]
+        idx = load("idx", [P, S // 16], U16, offs)
+        for q in range(4):
+            nc.sync.dma_start(tab_plane[32 * q : 32 * q + 8, :].bitcast(I32), tab_scales[:, 4 * q : 4 * q + 4, :].bitcast(I32))
+        w2_raw = held("w2_raw", [P, 2 * H], U8)
+        nc.sync.dma_start(w2_raw[:].bitcast(I32), w2_words[0].bitcast(I32))
+        w1_raw = {}
+        for a in range(2):
+            w1_raw[0, a] = load_wide(w1[a * KP : (a + 1) * KP, 0:KP])
+        tab_w.append(load_words("tab_w1", tab_words[1]))
+        for a in range(2):
+            w1_raw[1, a] = load_wide(w1[a * KP : (a + 1) * KP, KP : 2 * KP])
+        idx2 = load("idx2", [P, M // 16], U16, offs2)
+        tab2_w = load_words("tab2_w", tab2_words[0])
+        for q in range(4):
+            nc.sync.dma_start(tab2_plane[32 * q : 32 * q + 4, :].bitcast(I32), tab2_scales[0, 4 * q : 4 * q + 4, :].bitcast(I32))
+        for q in range(4):
+            nc.sync.dma_start(w2_plane[32 * q : 32 * q + 4, :].bitcast(I32), w2_scales[0, 4 * q : 4 * q + 4, :].bitcast(I32))
+        place = load("place", [P, M // 16], U16, pos1)
+        gains = load("gains", [P, 2, PACK], F32, gain.rearrange("(b p t) -> p b t", p=P, t=PACK))
+        shifts = [load("shift0", [P, PACK, M], F32, shift[0:KP, :].rearrange("(p t) m -> p t m", t=PACK))]
+        w3_raw = [load_wide(w3[b * KP : (b + 1) * KP, :]) for b in range(2)]
+        idx3 = load("idx3", [P, S // 16], U16, offs3)
+        wg1_sb = load("wg1_sb", [P, S], F32, wg1)
+        pages = [load("page0", [P, T], F32, page1[0:P, :])]
+        shifts.append(load("shift1", [P, PACK, M], F32, shift[KP : 2 * KP, :].rearrange("(p t) m -> p t m", t=PACK)))
+        pages.append(load("page1", [P, T], F32, page1[P : 2 * P, :]))
+        pages.append(load("page2", [P, T], F32, page1[2 * P : 3 * P, :]))
+        pages.append(load("page3", [P, T], F32, page1[3 * P : 4 * P, :]))
+        w4_w = held("w4_w", [P, 2, 2 * N], U8)
+        nc.sync.dma_start(w4_w[:].bitcast(I32), w4_words.rearrange("a p c -> p a c").bitcast(I32))
+        idx4 = load("idx4", [P, M // 16], U16, offs4)
+        wg2_sb = load("wg2_sb", [P, M], F32, wg2)
+
+        def grouped():
+            return ring.tile([P, PACK * W], BF16, name="grouped", bufs=3, align_bytes=64)
+
+        def quantize(src, codes, plane):
+            nc.vector.quantize_mx(out=codes[:].bitcast(FP8X4), scales=plane[:], in_=src[:])
+            return codes, plane
+
+        def copy_on(engine, dst, src):
+            if engine == "scalar":
+                nc.scalar.copy(dst, src)
+            else:
+                nc.vector.tensor_copy(dst, src)
+
+        def make_w1(b, a, engine):
+            g = grouped()
+            copy_on(
+                engine,
+                g[:].rearrange("p (t m j) -> p m j t", t=PACK, j=PACK),
+                w1_raw[b, a][:].rearrange("p j (m t) -> p m j t", t=PACK),
+            )
+            return quantize(g, held(f"w1_codes{b}{a}", [P, W], U32), held(f"w1_plane{b}{a}", [P, W], U8))
+
+        def interleave(engine, dst, src):
+            copy_on(
+                engine,
+                dst[:].rearrange("p (c i t) -> p c t i", i=4, t=PACK),
+                src[:].rearrange("p t (c i) -> p c t i", i=4),
+            )
+
+        def make_w3(b, engine):
+            g = grouped()
+            interleave(engine, g, w3_raw[b])
+            return quantize(g, held(f"w3_codes{b}", [P, W], U32), held(f"w3_plane{b}", [P, W], U8))
+
+        def bank(i):
+            return psum.tile([P, W], F32, name=f"bank{i}")
+
+        w2_w = held("w2_w", [P, 2 * H], U8)
+        nc.vector.tensor_copy(
+            w2_w[:].rearrange("p (b t m e) -> p b m t e", b=2, t=PACK, e=2),
+            w2_raw[:].rearrange("p (b m t e) -> p b m t e", b=2, t=PACK, e=2),
+        )
+        v_w = [held(f"v_w{a}", [P, S], U32) for a in range(2)]
+        v_plane = held("v_plane", [P, S], U8)
+        w1q = {}
+        nc.vector.tensor_copy(v_w[0][:], tab_w[0][:].indirect(idx[:]))
+        nc.vector.tensor_copy(v_plane[:], tab_plane[:].indirect(idx[:]))
+        w1q[0, 0] = make_w1(0, 0, "scalar")
+        w1q[0, 1] = make_w1(0, 1, "scalar")
+        for c in range(2):
+            nc.vector.tensor_copy(v_w[1][:, c * W : (c + 1) * W], tab_w[1][:].indirect(idx[:, c * LC : (c + 1) * LC]))
+        w2_s = held("w2_s", [P, H], U8)
+        nc.vector.tensor_copy(
+            w2_s[:].rearrange("p (b t m) -> p b m t", b=2, t=PACK),
+            w2_plane[:].rearrange("p (b m t) -> p b m t", b=2, t=PACK),
+        )
+
+        h1 = {(b, t): held(f"h1_{b}{t}", [P, S], F32) for b in range(2) for t in range(PACK)}
+
+        def h1_products(b, c, first_bank):
+            banks = []
+            cols = slice(c * W, (c + 1) * W)
+            for t in range(PACK):
+                acc = bank(first_bank + t)
+                rows = slice(t * P, (t + 1) * P)
+                for a in range(2):
+                    codes, plane = w1q[b, a]
+                    nc.tensor.matmul_mx(
+                        out=acc[:], lhsT=codes[:, rows].bitcast(FP8X4), lhsT_scale=plane[:, rows],
+                        rhs=v_w[a][:, cols].bitcast(FP8X4), rhs_scale=v_plane[4 * a :, cols],
+                        start=(a == 0), stop=(a == 1),
+                    )
+                banks.append(acc)
+            return banks
+
+        def keep_h1(b, c, banks):
+            for t in range(PACK):
+                nc.scalar.copy(h1[b, t][:, c * W : (c + 1) * W], banks[t][:])
+
+        def make_z(b, sources):
+            th = wide.tile([P, PACK, W], F32, name="wide", align_bytes=64)
+            for t in range(PACK):
+                nc.scalar.activation(th[:, t, :], sources[t], TANH)
+            planes = ring.tile([P, PACK, W], BF16, name="z_rows", bufs=2, align_bytes=64)
+            for t in range(PACK):
+                nc.scalar.activation(planes[:, t, :], th[:, t, :], COPY, scale=gains[:, b, t : t + 1])
+            g = grouped()
+            interleave("scalar", g, planes)
+            codes = ring.tile([P, W], U32, name="z_codes", bufs=4, align_bytes=64)
+            plane = ring.tile([P, W], U8, name="z_plane", bufs=4, align_bytes=64)
+            return quantize(g, codes, plane)
+
+        def h1_cols(b, c):
+            return [h1[b, t][:, c * W : (c + 1) * W] for t in range(PACK)]
+
+        def picked_plus_shift(b):
+            g = wide.tile([P, PACK, W], F32, name="wide", align_bytes=64)
+            for t in range(PACK):
+                nc.vector.tensor_tensor(g[:, t, :], h1[b, t][:].indirect(place[:]), shifts[b][:, t, :], ADD)
+            return g
+
+        def add_h2(b, g, first_bank):
+            for t in range(PACK):
+                acc = bank(first_bank + t)
+                c0 = b * KP + t * P
+                nc.tensor.matmul_mx(
+                    out=acc[:], lhsT=w2_w[:, 2 * c0 : 2 * (c0 + P)].bitcast(FP4X4), lhsT_scale=w2_s[:, c0 : c0 + P],
+                    rhs=v2_w[:].bitcast(FP8X4), rhs_scale=v2_plane[:], start=True, stop=True,
+                )
+                nc.vector.tensor_tensor(g[:, t, :], acc[:], g[:, t, :], ADD)
+            return [g[:, t, :] for t in range(PACK)]
+
+        def y_products(z, stationary, first_bank):
+            banks = []
+            for nb in range(N // P):
+                acc = bank(first_bank + nb)
+                for b in range(2):
+                    lhs, lhs_scale = stationary(b, nb)
+                    nc.tensor.matmul_mx(
+                        out=acc[:], lhsT=lhs, lhsT_scale=lhs_scale,
+                        rhs=z[b][0][:].bitcast(FP8X4), rhs_scale=z[b][1][:], start=(b == 0), stop=(b == 1),
+                    )
+                banks.append(acc)
+            return banks
+
+        def w3_block(b, nb):
+            cols = slice(nb * P, (nb + 1) * P)
+            return w3q[b][0][:, cols].bitcast(FP8X4), w3q[b][1][:, cols]
+
+        def w4_block(b, nb):
+            return w4_w[:, b, 2 * nb * P : 2 * (nb + 1) * P].bitcast(FP4X4), w4_plane[:, b, nb * P : (nb + 1) * P]
+
+        def put(nb, acc, offsets, weights):
+            y = ring.tile([P, W], F32, name="y", bufs=4, align_bytes=64)
+            nc.scalar.copy(y[:], acc[:])
+            nc.vector.tensor_tensor(pages[nb][:].indirect(offsets), y[:], weights, MULT)
+
+        X, Y = 0, 4
+        keep_h1(0, 0, h1_products(0, 0, X))
+        keep_h1(0, 1, h1_products(0, 1, Y))
+        w1q[1, 0] = make_w1(1, 0, "vector")
+        w1q[1, 1] = make_w1(1, 1, "vector")
+        v2_w = held("v2_w", [P, M], U32)
+        v2_plane = held("v2_plane", [P, M], U8)
+        nc.vector.tensor_copy(v2_w[:], tab2_w[:].indirect(idx2[:]))
+        nc.vector.tensor_copy(v2_plane[:], tab2_plane[:].indirect(idx2[:]))
+        g0 = picked_plus_shift(0)
+        w3q = [make_w3(b, "vector") for b in range(2)]
+
+        z10 = [make_z(0, h1_cols(0, 0))]
+        banks = h1_products(1, 0, X)
+        z10.append(make_z(1, [acc[:] for acc in banks]))
+        keep_h1(1, 0, banks)
+        pre0 = add_h2(0, g0, X)
+        y10 = y_products(z10, w3_block, Y)
+        for nb in range(3):
+            put(nb, y10[nb], idx3[:, 0:LC], wg1_sb[:, 0:W])
+
+        keep_h1(1, 1, h1_products(1, 1, X))
+        g1 = picked_plus_shift(1)
+        pre1 = add_h2(1, g1, X)
+        z11 = [make_z(b, h1_cols(b, 1)) for b in range(2)]
+        put(3, y10[3], idx3[:, 0:LC], wg1_sb[:, 0:W])
+        y11 = y_products(z11, w3_block, Y)
+        for nb in range(3):
+            put(nb, y11[nb], idx3[:, LC : 2 * LC], wg1_sb[:, W : 2 * W])
+
+        z2 = [make_z(0, pre0), make_z(1, pre1)]
+        put(3, y11[3], idx3[:, LC : 2 * LC], wg1_sb[:, W : 2 * W])
+        y2 = y_products(z2, w4_block, X)
+        for nb in range(4):
+            put(nb, y2[nb], idx4[:], wg2_sb[:])
+            nc.sync.dma_start(out[nb * P : (nb + 1) * P, :], pages[nb][:])

@@ -22,7 +22,10 @@ P = 128
 PACK = 4
 KP = P * PACK
 W = 512
-LC = W // 16
+LIST_COLS = W // 16
+QUADS = 4
+RUN = 4
+BANKS_A, BANKS_B = 0, 4
 
 
 def tile_list_trigger_features_kernel(
@@ -33,26 +36,48 @@ def tile_list_trigger_features_kernel(
     with ExitStack() as ctx:
         keep = ctx.enter_context(tc.tile_pool(name="keep", bufs=1))
         wide = ctx.enter_context(tc.tile_pool(name="wide", bufs=6))
+        rows = ctx.enter_context(tc.tile_pool(name="rows", bufs=5))
         ring = ctx.enter_context(tc.tile_pool(name="ring", bufs=1))
         psum = ctx.enter_context(tc.psum_pool(name="psum", bufs=1))
 
         def held(name, shape, dtype):
             return keep.tile(shape, dtype, name=name, align_bytes=64)
 
+        def wide_tile():
+            return wide.tile([P, PACK, W], F32, name="wide", align_bytes=64)
+
+        def grouped_tile():
+            return ring.tile([P, PACK * W], BF16, name="grouped", bufs=4, align_bytes=64)
+
+        def bank(i):
+            return psum.tile([P, W], F32, name=f"bank{i}")
+
         def load(name, shape, dtype, src):
-            t = held(name, shape, dtype)
-            nc.sync.dma_start(t[:], src)
-            return t
+            dst = held(name, shape, dtype)
+            nc.sync.dma_start(dst[:], src)
+            return dst
 
-        def load_wide(src):
-            t = wide.tile([P, PACK, W], F32, name="wide", align_bytes=64)
-            nc.sync.dma_start(t[:], src.rearrange("(p j) c -> p j c", j=PACK))
-            return t
+        def load_pass(src):
+            dst = wide_tile()
+            nc.sync.dma_start(dst[:], src.rearrange("(p j) c -> p j c", j=PACK))
+            return dst
 
-        def load_words(name, src):
-            t = held(name, [P, T], U32)
-            nc.sync.dma_start(t[:].bitcast(I32), src.rearrange("p t i -> p (t i)").bitcast(I32))
-            return t
+        def load_words(src):
+            dst = rows.tile([P, T], U32, name="rows", align_bytes=64)
+            nc.sync.dma_start(dst[:].bitcast(I32), src.rearrange("p t i -> p (t i)").bitcast(I32))
+            return dst
+
+        def load_page(nb):
+            dst = rows.tile([P, T], F32, name="rows", align_bytes=64)
+            nc.sync.dma_start(dst[:], page1[nb * P : (nb + 1) * P, :])
+            return dst
+
+        def load_w1(b, a):
+            return load_pass(w1[a * KP : (a + 1) * KP, b * KP : (b + 1) * KP])
+
+        def load_shift(b):
+            src = shift[b * KP : (b + 1) * KP, :].rearrange("(p t) m -> p t m", t=PACK)
+            return load(f"shift{b}", [P, PACK, M], F32, src)
 
         tab_plane = held("tab_plane", [P, T], U8)
         w2_plane = held("w2_plane", [P, H], U8)
@@ -62,82 +87,71 @@ def tile_list_trigger_features_kernel(
         nc.vector.memset(w2_plane[:].bitcast(I32), 0)
         nc.vector.memset(tab2_plane[:].bitcast(I32), 0)
         nc.vector.memset(w4_plane[:].bitcast(I32), 0)
-        for q in range(4):
+        for q in range(QUADS):
+            nc.gpsimd.dma_start(
+                w2_plane[32 * q : 32 * q + 4, :].bitcast(I32), w2_scales[0, 4 * q : 4 * q + 4, :].bitcast(I32)
+            )
+        for q in range(QUADS):
             nc.gpsimd.dma_start(
                 w4_plane[32 * q : 32 * q + 4, :, :].bitcast(I32),
                 w4_scales[:, 4 * q : 4 * q + 4, :].rearrange("a r n -> r a n").bitcast(I32),
             )
 
-        tab_w = [load_words("tab_w0", tab_words[0])]
         idx = load("idx", [P, S // 16], U16, offs)
-        for q in range(4):
-            nc.sync.dma_start(tab_plane[32 * q : 32 * q + 8, :].bitcast(I32), tab_scales[:, 4 * q : 4 * q + 4, :].bitcast(I32))
+        for q in range(QUADS):
+            nc.sync.dma_start(
+                tab_plane[32 * q : 32 * q + 8, :].bitcast(I32), tab_scales[:, 4 * q : 4 * q + 4, :].bitcast(I32)
+            )
+        tab_w = [load_words(tab_words[0])]
+        w1_raw = {(0, 0): load_w1(0, 0)}
         w2_raw = held("w2_raw", [P, 2 * H], U8)
         nc.sync.dma_start(w2_raw[:].bitcast(I32), w2_words[0].bitcast(I32))
-        w1_raw = {}
-        for a in range(2):
-            w1_raw[0, a] = load_wide(w1[a * KP : (a + 1) * KP, 0:KP])
-        tab_w.append(load_words("tab_w1", tab_words[1]))
-        for a in range(2):
-            w1_raw[1, a] = load_wide(w1[a * KP : (a + 1) * KP, KP : 2 * KP])
         idx2 = load("idx2", [P, M // 16], U16, offs2)
-        tab2_w = load_words("tab2_w", tab2_words[0])
-        for q in range(4):
-            nc.sync.dma_start(tab2_plane[32 * q : 32 * q + 4, :].bitcast(I32), tab2_scales[0, 4 * q : 4 * q + 4, :].bitcast(I32))
-        for q in range(4):
-            nc.sync.dma_start(w2_plane[32 * q : 32 * q + 4, :].bitcast(I32), w2_scales[0, 4 * q : 4 * q + 4, :].bitcast(I32))
+        for q in range(QUADS):
+            nc.sync.dma_start(
+                tab2_plane[32 * q : 32 * q + 4, :].bitcast(I32), tab2_scales[0, 4 * q : 4 * q + 4, :].bitcast(I32)
+            )
+        w1_raw[0, 1] = load_w1(0, 1)
+        tab_w.append(load_words(tab_words[1]))
+        w1_raw[1, 0] = load_w1(1, 0)
         place = load("place", [P, M // 16], U16, pos1)
+        w1_raw[1, 1] = load_w1(1, 1)
         gains = load("gains", [P, 2, PACK], F32, gain.rearrange("(b p t) -> p b t", p=P, t=PACK))
-        shifts = [load("shift0", [P, PACK, M], F32, shift[0:KP, :].rearrange("(p t) m -> p t m", t=PACK))]
-        w3_raw = [load_wide(w3[b * KP : (b + 1) * KP, :]) for b in range(2)]
+        shifts = [load_shift(0)]
+        tab2_w = load_words(tab2_words[0])
+        w3_raw = [load_pass(w3[b * KP : (b + 1) * KP, :]) for b in range(2)]
         idx3 = load("idx3", [P, S // 16], U16, offs3)
         wg1_sb = load("wg1_sb", [P, S], F32, wg1)
-        pages = [load("page0", [P, T], F32, page1[0:P, :])]
-        shifts.append(load("shift1", [P, PACK, M], F32, shift[KP : 2 * KP, :].rearrange("(p t) m -> p t m", t=PACK)))
-        pages.append(load("page1", [P, T], F32, page1[P : 2 * P, :]))
-        pages.append(load("page2", [P, T], F32, page1[2 * P : 3 * P, :]))
-        pages.append(load("page3", [P, T], F32, page1[3 * P : 4 * P, :]))
+        pages = [load_page(0)]
+        shifts.append(load_shift(1))
+        pages.extend([load_page(nb) for nb in range(1, N // P)])
         w4_w = held("w4_w", [P, 2, 2 * N], U8)
         nc.sync.dma_start(w4_w[:].bitcast(I32), w4_words.rearrange("a p c -> p a c").bitcast(I32))
         idx4 = load("idx4", [P, M // 16], U16, offs4)
         wg2_sb = load("wg2_sb", [P, M], F32, wg2)
 
-        def grouped():
-            return ring.tile([P, PACK * W], BF16, name="grouped", bufs=3, align_bytes=64)
-
         def quantize(src, codes, plane):
             nc.vector.quantize_mx(out=codes[:].bitcast(FP8X4), scales=plane[:], in_=src[:])
             return codes, plane
 
-        def copy_on(engine, dst, src):
-            if engine == "scalar":
-                nc.scalar.copy(dst, src)
-            else:
-                nc.vector.tensor_copy(dst, src)
+        def by_runs(grouped, four_rows):
+            return (
+                grouped[:].rearrange("p (c i t) -> p c t i", i=RUN, t=PACK),
+                four_rows[:].rearrange("p t (c i) -> p c t i", i=RUN),
+            )
 
-        def make_w1(b, a, engine):
-            g = grouped()
-            copy_on(
-                engine,
+        def make_w1(b, a, copy):
+            g = grouped_tile()
+            copy(
                 g[:].rearrange("p (t m j) -> p m j t", t=PACK, j=PACK),
                 w1_raw[b, a][:].rearrange("p j (m t) -> p m j t", t=PACK),
             )
             return quantize(g, held(f"w1_codes{b}{a}", [P, W], U32), held(f"w1_plane{b}{a}", [P, W], U8))
 
-        def interleave(engine, dst, src):
-            copy_on(
-                engine,
-                dst[:].rearrange("p (c i t) -> p c t i", i=4, t=PACK),
-                src[:].rearrange("p t (c i) -> p c t i", i=4),
-            )
-
-        def make_w3(b, engine):
-            g = grouped()
-            interleave(engine, g, w3_raw[b])
-            return quantize(g, held(f"w3_codes{b}", [P, W], U32), held(f"w3_plane{b}", [P, W], U8))
-
-        def bank(i):
-            return psum.tile([P, W], F32, name=f"bank{i}")
+        def make_w3(b, copy):
+            g = grouped_tile()
+            copy(*by_runs(g, w3_raw[b]))
+            return quantize(g, held(f"w3_codes{b}", [P, N], U32), held(f"w3_plane{b}", [P, N], U8))
 
         w2_w = held("w2_w", [P, 2 * H], U8)
         nc.vector.tensor_copy(
@@ -146,64 +160,45 @@ def tile_list_trigger_features_kernel(
         )
         v_w = [held(f"v_w{a}", [P, S], U32) for a in range(2)]
         v_plane = held("v_plane", [P, S], U8)
-        w1q = {}
-        nc.vector.tensor_copy(v_w[0][:], tab_w[0][:].indirect(idx[:]))
         nc.vector.tensor_copy(v_plane[:], tab_plane[:].indirect(idx[:]))
-        w1q[0, 0] = make_w1(0, 0, "scalar")
-        w1q[0, 1] = make_w1(0, 1, "scalar")
-        for c in range(2):
-            nc.vector.tensor_copy(v_w[1][:, c * W : (c + 1) * W], tab_w[1][:].indirect(idx[:, c * LC : (c + 1) * LC]))
+        nc.vector.tensor_copy(v_w[0][:], tab_w[0][:].indirect(idx[:]))
+        w1q = {(0, a): make_w1(0, a, nc.scalar.copy) for a in range(2)}
+        for c in range(S // W):
+            nc.vector.tensor_copy(
+                v_w[1][:, c * W : (c + 1) * W], tab_w[1][:].indirect(idx[:, c * LIST_COLS : (c + 1) * LIST_COLS])
+            )
         w2_s = held("w2_s", [P, H], U8)
-        nc.vector.tensor_copy(
+        nc.gpsimd.tensor_copy(
             w2_s[:].rearrange("p (b t m) -> p b m t", b=2, t=PACK),
             w2_plane[:].rearrange("p (b m t) -> p b m t", b=2, t=PACK),
         )
 
         h1 = {(b, t): held(f"h1_{b}{t}", [P, S], F32) for b in range(2) for t in range(PACK)}
 
-        def h1_products(b, c, first_bank):
-            banks = []
+        def make_h1(b, c, first_bank):
             cols = slice(c * W, (c + 1) * W)
+            banks = []
             for t in range(PACK):
                 acc = bank(first_bank + t)
-                rows = slice(t * P, (t + 1) * P)
+                lhs = slice(t * P, (t + 1) * P)
                 for a in range(2):
                     codes, plane = w1q[b, a]
                     nc.tensor.matmul_mx(
-                        out=acc[:], lhsT=codes[:, rows].bitcast(FP8X4), lhsT_scale=plane[:, rows],
+                        out=acc[:], lhsT=codes[:, lhs].bitcast(FP8X4), lhsT_scale=plane[:, lhs],
                         rhs=v_w[a][:, cols].bitcast(FP8X4), rhs_scale=v_plane[4 * a :, cols],
                         start=(a == 0), stop=(a == 1),
                     )
                 banks.append(acc)
-            return banks
-
-        def keep_h1(b, c, banks):
             for t in range(PACK):
-                nc.scalar.copy(h1[b, t][:, c * W : (c + 1) * W], banks[t][:])
-
-        def make_z(b, sources):
-            th = wide.tile([P, PACK, W], F32, name="wide", align_bytes=64)
-            for t in range(PACK):
-                nc.scalar.activation(th[:, t, :], sources[t], TANH)
-            planes = ring.tile([P, PACK, W], BF16, name="z_rows", bufs=2, align_bytes=64)
-            for t in range(PACK):
-                nc.scalar.activation(planes[:, t, :], th[:, t, :], COPY, scale=gains[:, b, t : t + 1])
-            g = grouped()
-            interleave("scalar", g, planes)
-            codes = ring.tile([P, W], U32, name="z_codes", bufs=4, align_bytes=64)
-            plane = ring.tile([P, W], U8, name="z_plane", bufs=4, align_bytes=64)
-            return quantize(g, codes, plane)
-
-        def h1_cols(b, c):
-            return [h1[b, t][:, c * W : (c + 1) * W] for t in range(PACK)]
+                nc.scalar.copy(h1[b, t][:, cols], banks[t][:])
 
         def picked_plus_shift(b):
-            g = wide.tile([P, PACK, W], F32, name="wide", align_bytes=64)
+            total = wide_tile()
             for t in range(PACK):
-                nc.vector.tensor_tensor(g[:, t, :], h1[b, t][:].indirect(place[:]), shifts[b][:, t, :], ADD)
-            return g
+                nc.vector.tensor_tensor(total[:, t, :], h1[b, t][:].indirect(place[:]), shifts[b][:, t, :], ADD)
+            return total
 
-        def add_h2(b, g, first_bank):
+        def add_h2(b, total, first_bank):
             for t in range(PACK):
                 acc = bank(first_bank + t)
                 c0 = b * KP + t * P
@@ -211,21 +206,29 @@ def tile_list_trigger_features_kernel(
                     out=acc[:], lhsT=w2_w[:, 2 * c0 : 2 * (c0 + P)].bitcast(FP4X4), lhsT_scale=w2_s[:, c0 : c0 + P],
                     rhs=v2_w[:].bitcast(FP8X4), rhs_scale=v2_plane[:], start=True, stop=True,
                 )
-                nc.vector.tensor_tensor(g[:, t, :], acc[:], g[:, t, :], ADD)
-            return [g[:, t, :] for t in range(PACK)]
+                nc.vector.tensor_tensor(total[:, t, :], acc[:], total[:, t, :], ADD)
+            return [total[:, t, :] for t in range(PACK)]
 
-        def y_products(z, stationary, first_bank):
-            banks = []
-            for nb in range(N // P):
-                acc = bank(first_bank + nb)
-                for b in range(2):
-                    lhs, lhs_scale = stationary(b, nb)
-                    nc.tensor.matmul_mx(
-                        out=acc[:], lhsT=lhs, lhsT_scale=lhs_scale,
-                        rhs=z[b][0][:].bitcast(FP8X4), rhs_scale=z[b][1][:], start=(b == 0), stop=(b == 1),
-                    )
-                banks.append(acc)
-            return banks
+        def h1_chunk(b, c):
+            return [h1[b, t][:, c * W : (c + 1) * W] for t in range(PACK)]
+
+        def make_z(b, args, gain_on_vector=False):
+            th = wide_tile()
+            for t in range(PACK):
+                nc.scalar.activation(th[:, t, :], args[t], TANH)
+            g = grouped_tile()
+            if gain_on_vector:
+                dst, src = by_runs(g, th)
+                spread = gains[:, b, :].unsqueeze(1).unsqueeze(3).to_broadcast([P, W // RUN, PACK, RUN])
+                nc.vector.tensor_tensor(dst, src, spread, MULT)
+            else:
+                z_rows = ring.tile([P, PACK, W], BF16, name="z_rows", bufs=2, align_bytes=64)
+                for t in range(PACK):
+                    nc.scalar.activation(z_rows[:, t, :], th[:, t, :], COPY, scale=gains[:, b, t : t + 1])
+                nc.scalar.copy(*by_runs(g, z_rows))
+            codes = ring.tile([P, W], U32, name="z_codes", bufs=4, align_bytes=64)
+            plane = ring.tile([P, W], U8, name="z_plane", bufs=4, align_bytes=64)
+            return quantize(g, codes, plane)
 
         def w3_block(b, nb):
             cols = slice(nb * P, (nb + 1) * P)
@@ -234,44 +237,56 @@ def tile_list_trigger_features_kernel(
         def w4_block(b, nb):
             return w4_w[:, b, 2 * nb * P : 2 * (nb + 1) * P].bitcast(FP4X4), w4_plane[:, b, nb * P : (nb + 1) * P]
 
+        def make_y(z, weight_block, first_bank):
+            banks = []
+            for nb in range(N // P):
+                acc = bank(first_bank + nb)
+                for b in range(2):
+                    lhs, lhs_scale = weight_block(b, nb)
+                    nc.tensor.matmul_mx(
+                        out=acc[:], lhsT=lhs, lhsT_scale=lhs_scale,
+                        rhs=z[b][0][:].bitcast(FP8X4), rhs_scale=z[b][1][:], start=(b == 0), stop=(b == 1),
+                    )
+                banks.append(acc)
+            return banks
+
         def put(nb, acc, offsets, weights):
-            y = ring.tile([P, W], F32, name="y", bufs=4, align_bytes=64)
+            y = ring.tile([P, W], F32, name="y", bufs=6, align_bytes=64)
             nc.scalar.copy(y[:], acc[:])
             nc.vector.tensor_tensor(pages[nb][:].indirect(offsets), y[:], weights, MULT)
 
-        X, Y = 0, 4
-        keep_h1(0, 0, h1_products(0, 0, X))
-        keep_h1(0, 1, h1_products(0, 1, Y))
-        w1q[1, 0] = make_w1(1, 0, "vector")
-        w1q[1, 1] = make_w1(1, 1, "vector")
+        make_h1(0, 0, BANKS_A)
+        make_h1(0, 1, BANKS_B)
+        for a in range(2):
+            w1q[1, a] = make_w1(1, a, nc.vector.tensor_copy)
+        make_h1(1, 0, BANKS_A)
+        total0 = picked_plus_shift(0)
         v2_w = held("v2_w", [P, M], U32)
         v2_plane = held("v2_plane", [P, M], U8)
         nc.vector.tensor_copy(v2_w[:], tab2_w[:].indirect(idx2[:]))
         nc.vector.tensor_copy(v2_plane[:], tab2_plane[:].indirect(idx2[:]))
-        g0 = picked_plus_shift(0)
-        w3q = [make_w3(b, "vector") for b in range(2)]
+        w3q = [make_w3(0, nc.vector.tensor_copy)]
+        z2_args = [add_h2(0, total0, BANKS_A)]
+        z = [make_z(0, h1_chunk(0, 0)), make_z(1, h1_chunk(1, 0), gain_on_vector=True)]
+        w3q.append(make_w3(1, nc.scalar.copy))
+        make_h1(1, 1, BANKS_B)
+        z2_args.append(add_h2(1, picked_plus_shift(1), BANKS_B))
 
-        z10 = [make_z(0, h1_cols(0, 0))]
-        banks = h1_products(1, 0, X)
-        z10.append(make_z(1, [acc[:] for acc in banks]))
-        keep_h1(1, 0, banks)
-        pre0 = add_h2(0, g0, X)
-        y10 = y_products(z10, w3_block, Y)
-        for nb in range(3):
-            put(nb, y10[nb], idx3[:, 0:LC], wg1_sb[:, 0:W])
-
-        keep_h1(1, 1, h1_products(1, 1, X))
-        g1 = picked_plus_shift(1)
-        pre1 = add_h2(1, g1, X)
-        z11 = [make_z(b, h1_cols(b, 1)) for b in range(2)]
-        put(3, y10[3], idx3[:, 0:LC], wg1_sb[:, 0:W])
-        y11 = y_products(z11, w3_block, Y)
-        for nb in range(3):
-            put(nb, y11[nb], idx3[:, LC : 2 * LC], wg1_sb[:, W : 2 * W])
-
-        z2 = [make_z(0, pre0), make_z(1, pre1)]
-        put(3, y11[3], idx3[:, LC : 2 * LC], wg1_sb[:, W : 2 * W])
-        y2 = y_products(z2, w4_block, X)
-        for nb in range(4):
-            put(nb, y2[nb], idx4[:], wg2_sb[:])
-            nc.sync.dma_start(out[nb * P : (nb + 1) * P, :], pages[nb][:])
+        chunks = [
+            (w3_block, idx3[:, 0:LIST_COLS], wg1_sb[:, 0:W]),
+            (w3_block, idx3[:, LIST_COLS : 2 * LIST_COLS], wg1_sb[:, W : 2 * W]),
+            (w4_block, idx4[:], wg2_sb[:]),
+        ]
+        next_args = [[h1_chunk(b, 1) for b in range(2)], z2_args]
+        for n, (weight_block, offsets, weights) in enumerate(chunks):
+            y_banks = make_y(z, weight_block, (BANKS_A, BANKS_B)[n % 2])
+            if n < len(next_args):
+                z = []
+                for b in range(2):
+                    z.append(make_z(b, next_args[n][b]))
+                    for nb in (2 * b, 2 * b + 1):
+                        put(nb, y_banks[nb], offsets, weights)
+            else:
+                for nb in range(N // P):
+                    put(nb, y_banks[nb], offsets, weights)
+                    nc.sync.dma_start(out[nb * P : (nb + 1) * P, :], pages[nb][:])

@@ -143,8 +143,8 @@ def tile_list_trigger_features_kernel(
         def make_w1(b, a, copy):
             g = grouped_tile()
             copy(
-                g[:].rearrange("p (t m j) -> p m j t", t=PACK, j=PACK),
-                w1_raw[b, a][:].rearrange("p j (m t) -> p m j t", t=PACK),
+                g[:].rearrange("p (u e m j) -> p u m j e", u=2, e=2, j=PACK),
+                w1_raw[b, a][:].rearrange("p j (m u e) -> p u m j e", u=2, e=2),
             )
             return quantize(g, held(f"w1_codes{b}{a}", [P, W], U32), held(f"w1_plane{b}{a}", [P, W], U8))
 

@@ -91,11 +91,6 @@ def tile_list_trigger_features_kernel(
             nc.gpsimd.dma_start(
                 w2_plane[32 * q : 32 * q + 4, :].bitcast(I32), w2_scales[0, 4 * q : 4 * q + 4, :].bitcast(I32)
             )
-        for q in range(QUADS):
-            nc.gpsimd.dma_start(
-                w4_plane[32 * q : 32 * q + 4, :, :].bitcast(I32),
-                w4_scales[:, 4 * q : 4 * q + 4, :].rearrange("a r n -> r a n").bitcast(I32),
-            )
 
         idx = load("idx", [P, S // 16], U16, offs)
         for q in range(QUADS):
@@ -127,6 +122,11 @@ def tile_list_trigger_features_kernel(
         pages.extend([load_page(nb) for nb in range(1, N // P)])
         w4_w = held("w4_w", [P, 2, 2 * N], U8)
         nc.sync.dma_start(w4_w[:].bitcast(I32), w4_words.rearrange("a p c -> p a c").bitcast(I32))
+        for q in range(QUADS):
+            nc.sync.dma_start(
+                w4_plane[32 * q : 32 * q + 4, :, :].bitcast(I32),
+                w4_scales[:, 4 * q : 4 * q + 4, :].rearrange("a r n -> r a n").bitcast(I32),
+            )
         idx4 = load("idx4", [P, M // 16], U16, offs4)
         wg2_sb = load("wg2_sb", [P, M], F32, wg2)
 
@@ -265,10 +265,9 @@ def tile_list_trigger_features_kernel(
         v2_plane = held("v2_plane", [P, M], U8)
         nc.vector.tensor_copy(v2_w[:], tab2_w[:].indirect(idx2[:]))
         nc.vector.tensor_copy(v2_plane[:], tab2_plane[:].indirect(idx2[:]))
-        w3q = [make_w3(0, nc.vector.tensor_copy)]
+        w3q = [make_w3(b, nc.vector.tensor_copy) for b in range(2)]
         z2_args = [add_h2(0, total0, BANKS_A)]
         z = [make_z(0, h1_chunk(0, 0)), make_z(1, h1_chunk(1, 0), gain_on_vector=True)]
-        w3q.append(make_w3(1, nc.scalar.copy))
         make_h1(1, 1, BANKS_B)
         z2_args.append(add_h2(1, picked_plus_shift(1), BANKS_B))
 

from contextlib import ExitStack

import concourse.mybir as mybir

K1, K2, H, N, T, S, M = 1024, 512, 1024, 512, 2048, 1024, 512
FLOPS = 2 * (K1 * H * S + K2 * H * M + H * N * S + H * N * M)

F32 = mybir.dt.float32
BF16 = mybir.dt.bfloat16
I32 = mybir.dt.int32
U32 = mybir.dt.uint32
U16 = mybir.dt.uint16
U8 = mybir.dt.uint8
FP8X4 = mybir.dt.float8_e4m3fn_x4
FP4X4 = mybir.dt.float4_e2m1fn_x4
ADD = mybir.AluOpType.add
MULT = mybir.AluOpType.mult
TANH = mybir.ActivationFunctionType.Tanh
COPY = mybir.ActivationFunctionType.Copy

P = 128
PACK = 4
KP = P * PACK
W = 512
LIST_COLS = W // 16
QUADS = 4
RUN = 4
BANKS_A, BANKS_B = 0, 4


def tile_list_trigger_features_kernel(
    tc, tab_words, tab_scales, tab2_words, tab2_scales, offs, offs2, pos1, offs3, offs4,
    w1, w2_words, w2_scales, shift, gain, w3, w4_words, w4_scales, page1, wg1, wg2, out,
):
    nc = tc.nc
    with ExitStack() as ctx:
        keep = ctx.enter_context(tc.tile_pool(name="keep", bufs=1))
        wide = ctx.enter_context(tc.tile_pool(name="wide", bufs=6))
        rows = ctx.enter_context(tc.tile_pool(name="rows", bufs=5))
        ring = ctx.enter_context(tc.tile_pool(name="ring", bufs=1))
        psum = ctx.enter_context(tc.psum_pool(name="psum", bufs=1))

        def held(name, shape, dtype):
            return keep.tile(shape, dtype, name=name, align_bytes=64)

        def wide_tile():
            return wide.tile([P, PACK, W], F32, name="wide", align_bytes=64)

        def grouped_tile():
            return ring.tile([P, PACK * W], BF16, name="grouped", bufs=4, align_bytes=64)

        def bank(i):
            return psum.tile([P, W], F32, name=f"bank{i}")

        def load(name, shape, dtype, src):
            dst = held(name, shape, dtype)
            nc.sync.dma_start(dst[:], src)
            return dst

        def load_pass(src):
            dst = wide_tile()
            nc.sync.dma_start(dst[:], src.rearrange("(p j) c -> p j c", j=PACK))
            return dst

        def load_words(src):
            dst = rows.tile([P, T], U32, name="rows", align_bytes=64)
            nc.sync.dma_start(dst[:].bitcast(I32), src.rearrange("p t i -> p (t i)").bitcast(I32))
            return dst

        def load_page(nb):
            dst = rows.tile([P, T], F32, name="rows", align_bytes=64)
            nc.sync.dma_start(dst[:], page1[nb * P : (nb + 1) * P, :])
            return dst

        def load_w1(b, a):
            return load_pass(w1[a * KP : (a + 1) * KP, b * KP : (b + 1) * KP])

        def load_shift(b):
            src = shift[b * KP : (b + 1) * KP, :].rearrange("(p t) m -> p t m", t=PACK)
            return load(f"shift{b}", [P, PACK, M], F32, src)

        tab_plane = held("tab_plane", [P, T], U8)
        w2_plane = held("w2_plane", [P, H], U8)
        tab2_plane = held("tab2_plane", [P, T], U8)
        w4_plane = held("w4_plane", [P, 2, N], U8)
        nc.gpsimd.memset(tab_plane[:].bitcast(I32), 0)
        nc.vector.memset(w2_plane[:].bitcast(I32), 0)
        nc.vector.memset(tab2_plane[:].bitcast(I32), 0)
        nc.vector.memset(w4_plane[:].bitcast(I32), 0)
        for q in range(QUADS):
            nc.gpsimd.dma_start(
                w2_plane[32 * q : 32 * q + 4, :].bitcast(I32), w2_scales[0, 4 * q : 4 * q + 4, :].bitcast(I32)
            )

        idx = load("idx", [P, S // 16], U16, offs)
        for q in range(QUADS):
            nc.sync.dma_start(
                tab_plane[32 * q : 32 * q + 8, :].bitcast(I32), tab_scales[:, 4 * q : 4 * q + 4, :].bitcast(I32)
            )
        tab_w = [load_words(tab_words[0])]
        w1_raw = {(0, 0): load_w1(0, 0)}
        w2_raw = held("w2_raw", [P, 2 * H], U8)
        nc.sync.dma_start(w2_raw[:].bitcast(I32), w2_words[0].bitcast(I32))
        idx2 = load("idx2", [P, M // 16], U16, offs2)
        for q in range(QUADS):
            nc.sync.dma_start(
                tab2_plane[32 * q : 32 * q + 4, :].bitcast(I32), tab2_scales[0, 4 * q : 4 * q + 4, :].bitcast(I32)
            )
        w1_raw[0, 1] = load_w1(0, 1)
        tab_w.append(load_words(tab_words[1]))
        w1_raw[1, 0] = load_w1(1, 0)
        place = load("place", [P, M // 16], U16, pos1)
        w1_raw[1, 1] = load_w1(1, 1)
        gains = load("gains", [P, 2, PACK], F32, gain.rearrange("(b p t) -> p b t", p=P, t=PACK))
        shifts = [load_shift(0)]
        tab2_w = load_words(tab2_words[0])
        w3_raw = [load_pass(w3[b * KP : (b + 1) * KP, :]) for b in range(2)]
        idx3 = load("idx3", [P, S // 16], U16, offs3)
        wg1_sb = load("wg1_sb", [P, S], F32, wg1)
        pages = [load_page(0)]
        shifts.append(load_shift(1))
        pages.extend([load_page(nb) for nb in range(1, N // P)])
        w4_w = held("w4_w", [P, 2, 2 * N], U8)
        nc.sync.dma_start(w4_w[:].bitcast(I32), w4_words.rearrange("a p c -> p a c").bitcast(I32))
        for q in range(QUADS):
            nc.sync.dma_start(
                w4_plane[32 * q : 32 * q + 4, :, :].bitcast(I32),
                w4_scales[:, 4 * q : 4 * q + 4, :].rearrange("a r n -> r a n").bitcast(I32),
            )
        idx4 = load("idx4", [P, M // 16], U16, offs4)
        wg2_sb = load("wg2_sb", [P, M], F32, wg2)

        def quantize(src, codes, plane):
            nc.vector.quantize_mx(out=codes[:].bitcast(FP8X4), scales=plane[:], in_=src[:])
            return codes, plane

        def by_runs(grouped, four_rows):
            return (
                grouped[:].rearrange("p (c i t) -> p c t i", i=RUN, t=PACK),
                four_rows[:].rearrange("p t (c i) -> p c t i", i=RUN),
            )

        def make_w1(b, a, copy):
            g = grouped_tile()
            copy(
                g[:].rearrange("p (u e m j) -> p u m j e", u=2, e=2, j=PACK),
                w1_raw[b, a][:].rearrange("p j (m u e) -> p u m j e", u=2, e=2),
            )
            return quantize(g, held(f"w1_codes{b}{a}", [P, W], U32), held(f"w1_plane{b}{a}", [P, W], U8))

        def make_w3(b, copy):
            g = grouped_tile()
            copy(*by_runs(g, w3_raw[b]))
            return quantize(g, held(f"w3_codes{b}", [P, N], U32), held(f"w3_plane{b}", [P, N], U8))

        w2_w = held("w2_w", [P, 2 * H], U8)
        nc.vector.tensor_copy(
            w2_w[:].rearrange("p (b t m e) -> p b m t e", b=2, t=PACK, e=2),
            w2_raw[:].rearrange("p (b m t e) -> p b m t e", b=2, t=PACK, e=2),
        )
        v_w = [held(f"v_w{a}", [P, S], U32) for a in range(2)]
        v_plane = held("v_plane", [P, S], U8)
        nc.vector.tensor_copy(v_plane[:], tab_plane[:].indirect(idx[:]))
        nc.vector.tensor_copy(v_w[0][:], tab_w[0][:].indirect(idx[:]))
        w1q = {(0, a): make_w1(0, a, nc.scalar.copy) for a in range(2)}
        for c in range(S // W):
            nc.vector.tensor_copy(
                v_w[1][:, c * W : (c + 1) * W], tab_w[1][:].indirect(idx[:, c * LIST_COLS : (c + 1) * LIST_COLS])
            )
        w2_s = held("w2_s", [P, H], U8)
        nc.gpsimd.tensor_copy(
            w2_s[:].rearrange("p (b t m) -> p b m t", b=2, t=PACK),
            w2_plane[:].rearrange("p (b m t) -> p b m t", b=2, t=PACK),
        )

        h1 = {(b, t): held(f"h1_{b}{t}", [P, S], F32) for b in range(2) for t in range(PACK)}

        def make_h1(b, c, first_bank):
            cols = slice(c * W, (c + 1) * W)
            banks = []
            for t in range(PACK):
                acc = bank(first_bank + t)
                lhs = slice(t * P, (t + 1) * P)
                for a in range(2):
                    codes, plane = w1q[b, a]
                    nc.tensor.matmul_mx(
                        out=acc[:], lhsT=codes[:, lhs].bitcast(FP8X4), lhsT_scale=plane[:, lhs],
                        rhs=v_w[a][:, cols].bitcast(FP8X4), rhs_scale=v_plane[4 * a :, cols],
                        start=(a == 0), stop=(a == 1),
                    )
                banks.append(acc)
            for t in range(PACK):
                nc.scalar.copy(h1[b, t][:, cols], banks[t][:])

        def picked_plus_shift(b):
            total = wide_tile()
            for t in range(PACK):
                nc.vector.tensor_tensor(total[:, t, :], h1[b, t][:].indirect(place[:]), shifts[b][:, t, :], ADD)
            return total

        def add_h2(b, total, first_bank):
            for t in range(PACK):
                acc = bank(first_bank + t)
                c0 = b * KP + t * P
                nc.tensor.matmul_mx(
                    out=acc[:], lhsT=w2_w[:, 2 * c0 : 2 * (c0 + P)].bitcast(FP4X4), lhsT_scale=w2_s[:, c0 : c0 + P],
                    rhs=v2_w[:].bitcast(FP8X4), rhs_scale=v2_plane[:], start=True, stop=True,
                )
                nc.vector.tensor_tensor(total[:, t, :], acc[:], total[:, t, :], ADD)
            return [total[:, t, :] for t in range(PACK)]

        def h1_chunk(b, c):
            return [h1[b, t][:, c * W : (c + 1) * W] for t in range(PACK)]

        def make_z(b, args, gain_on_vector=False):
            th = wide_tile()
            for t in range(PACK):
                nc.scalar.activation(th[:, t, :], args[t], TANH)
            g = grouped_tile()
            if gain_on_vector:
                dst, src = by_runs(g, th)
                spread = gains[:, b, :].unsqueeze(1).unsqueeze(3).to_broadcast([P, W // RUN, PACK, RUN])
                nc.vector.tensor_tensor(dst, src, spread, MULT)
            else:
                z_rows = ring.tile([P, PACK, W], BF16, name="z_rows", bufs=2, align_bytes=64)
                for t in range(PACK):
                    nc.scalar.activation(z_rows[:, t, :], th[:, t, :], COPY, scale=gains[:, b, t : t + 1])
                nc.scalar.copy(*by_runs(g, z_rows))
            codes = ring.tile([P, W], U32, name="z_codes", bufs=4, align_bytes=64)
            plane = ring.tile([P, W], U8, name="z_plane", bufs=4, align_bytes=64)
            return quantize(g, codes, plane)

        def w3_block(b, nb):
            cols = slice(nb * P, (nb + 1) * P)
            return w3q[b][0][:, cols].bitcast(FP8X4), w3q[b][1][:, cols]

        def w4_block(b, nb):
            return w4_w[:, b, 2 * nb * P : 2 * (nb + 1) * P].bitcast(FP4X4), w4_plane[:, b, nb * P : (nb + 1) * P]

        def make_y(z, weight_block, first_bank):
            banks = []
            for nb in range(N // P):
                acc = bank(first_bank + nb)
                for b in range(2):
                    lhs, lhs_scale = weight_block(b, nb)
                    nc.tensor.matmul_mx(
                        out=acc[:], lhsT=lhs, lhsT_scale=lhs_scale,
                        rhs=z[b][0][:].bitcast(FP8X4), rhs_scale=z[b][1][:], start=(b == 0), stop=(b == 1),
                    )
                banks.append(acc)
            return banks

        def put(nb, acc, offsets, weights):
            y = ring.tile([P, W], F32, name="y", bufs=6, align_bytes=64)
            nc.scalar.copy(y[:], acc[:])
            nc.vector.tensor_tensor(pages[nb][:].indirect(offsets), y[:], weights, MULT)

        make_h1(0, 0, BANKS_A)
        make_h1(0, 1, BANKS_B)
        for a in range(2):
            w1q[1, a] = make_w1(1, a, nc.vector.tensor_copy)
        make_h1(1, 0, BANKS_A)
        total0 = picked_plus_shift(0)
        v2_w = held("v2_w", [P, M], U32)
        v2_plane = held("v2_plane", [P, M], U8)
        nc.vector.tensor_copy(v2_w[:], tab2_w[:].indirect(idx2[:]))
        nc.vector.tensor_copy(v2_plane[:], tab2_plane[:].indirect(idx2[:]))
        w3q = [make_w3(b, nc.vector.tensor_copy) for b in range(2)]
        z2_args = [add_h2(0, total0, BANKS_A)]
        z = [make_z(0, h1_chunk(0, 0)), make_z(1, h1_chunk(1, 0), gain_on_vector=True)]
        make_h1(1, 1, BANKS_B)
        z2_args.append(add_h2(1, picked_plus_shift(1), BANKS_B))

        chunks = [
            (w3_block, idx3[:, 0:LIST_COLS], wg1_sb[:, 0:W]),
            (w3_block, idx3[:, LIST_COLS : 2 * LIST_COLS], wg1_sb[:, W : 2 * W]),
            (w4_block, idx4[:], wg2_sb[:]),
        ]
        next_args = [[h1_chunk(b, 1) for b in range(2)], z2_args]
        for n, (weight_block, offsets, weights) in enumerate(chunks):
            y_banks = make_y(z, weight_block, (BANKS_A, BANKS_B)[n % 2])
            if n < len(next_args):
                z = []
                for b in range(2):
                    z.append(make_z(b, next_args[n][b]))
                    for nb in (2 * b, 2 * b + 1):
                        put(nb, y_banks[nb], offsets, weights)
            else:
                for nb in range(N // P):
                    put(nb, y_banks[nb], offsets, weights)
                    nc.sync.dma_start(out[nb * P : (nb + 1) * P, :], pages[nb][:])
